import numpy as np
import ml_dtypes


def mxq(x, axis, fmt="e4m3"):
    dtype, down = {"e4m3": (ml_dtypes.float8_e4m3fn, 7), "e5m2": (ml_dtypes.float8_e5m2, 14)}[fmt]
    v = np.moveaxis(np.asarray(x, np.float32).astype(ml_dtypes.bfloat16).astype(np.float64), axis, -1)
    blocks = v.reshape(v.shape[:-1] + (-1, 32))
    amax = np.abs(blocks).max(-1, keepdims=True)
    byte = np.maximum(np.where(amax > 0, np.frexp(amax)[1] - 1 + 127, 0) - down, 1)
    scale = np.exp2(byte - 127.0)
    codes = (blocks / scale).astype(np.float32).astype(dtype).astype(np.float64)
    return np.moveaxis((codes * scale).reshape(v.shape), -1, axis)


WIDE = False


def mx_kscale(k):
    if not WIDE:
        return np.ones(k)
    levels = np.array([10, -10, 5, -5, 0])
    if k % 512:
        return np.exp2(np.random.permutation(np.resize(levels, k // 32))).repeat(32)
    a = np.empty((k // 512, 16))
    for p in range(k // 512):
        a[p, :8] = np.random.permutation(np.resize(levels, 8))
        for g in range(8):
            far = levels[np.abs(levels - a[p, g]) >= 10]
            a[p, g + 8] = far[np.random.randint(len(far))]
    return np.exp2(a.ravel()).repeat(32)


def f64(x):
    return np.asarray(x).astype(np.float64)


def striped(idx):
    return np.tile(np.asarray(idx).reshape(-1, 16).T, (8, 1)).astype(np.uint16)


def unstriped(offs):
    return offs[:16].T.reshape(-1).astype(np.int64)


E2M1 = np.array([0.0, 0.5, 1.0, 1.5, 2.0, 3.0, 4.0, 6.0, -0.0, -0.5, -1.0, -1.5, -2.0, -3.0, -4.0, -6.0])


def pack_weight(w, fmt):
    k, n = w.shape
    w = f64(np.asarray(w, np.float32).astype(ml_dtypes.bfloat16)).reshape(k // 32, 32, n)
    amax = np.abs(w).max(1)
    if fmt == "e4m3":
        byte = np.frexp(amax)[1] - 1 + 127 - 7
    else:
        mant, ex = np.frexp(amax / 6.0)
        byte = np.where(mant > 0.5, ex, ex - 1) + 127
    byte = np.clip(np.where(amax > 0, byte, 1), 1, 254)
    scaled = (w * np.exp2(127.0 - byte)[:, None, :]).reshape(k, n).astype(np.float32)
    by_word = np.ascontiguousarray(scaled.reshape(k // 512, 128, 4, n).transpose(0, 1, 3, 2))
    if fmt == "e4m3":
        words = by_word.astype(ml_dtypes.float8_e4m3fn).view(np.uint8)
    else:
        c = by_word.astype(ml_dtypes.float4_e2m1fn).view(np.uint8) & 0xF
        words = (c[..., 0::2] | (c[..., 1::2] << 4)).reshape(k // 512, 128, 2 * n)
    return np.ascontiguousarray(words), np.ascontiguousarray(byte.astype(np.uint8).reshape(k // 512, 16, n))


def unpack_weight(words, scales, fmt):
    g, _, n = scales.shape
    words = np.ascontiguousarray(words).reshape(g, 128, n, -1)
    if fmt == "e4m3":
        vals = words.view(ml_dtypes.float8_e4m3fn).astype(np.float64)
    else:
        nib = np.empty((g, 128, n, 4), np.uint8)
        nib[..., 0::2] = words & 0xF
        nib[..., 1::2] = words >> 4
        vals = E2M1[nib]
    vals = vals * np.repeat(np.exp2(scales.astype(np.float64) - 127.0), 8, axis=1)[..., None]
    return vals.transpose(0, 1, 3, 2).reshape(g * 512, n)


B, N, T, D, DV, NQ = 2, 512, 2048, 1024, 256, 128
PAGE = 64


def setup_inputs():
    n = np.random.standard_normal
    pages = np.random.permutation(T // PAGE)[:B * N // PAGE]
    idx = (pages[:, None] * PAGE + np.arange(PAGE)[None, :]).reshape(-1)
    s = mx_kscale(D)[:, None]
    u = np.ones(T)
    u[idx] = mx_kscale(B * N)
    r = np.random.uniform(0.5, 2.0, T)
    k = n((D, T)) / s
    v = n((DV, T)) / (u * r)
    kp = pack_weight(k, "e2m1")
    return {
        "qT": (n((B, D, NQ)) * s * (1.00 / np.sqrt(D))).astype(np.float32),
        "k_words": np.ascontiguousarray(kp[0].reshape(D // 1024, 2, 128, T, 2).transpose(0, 2, 3, 1, 4)).reshape(D // 1024, 128, T, 4),
        "k_scales": kp[1],
        "vT": v.astype(np.float32),
        "vs": np.tile(u * r, (128, 1)).astype(np.float32),
        "offs": striped(idx),
    }


def reference(qT, k_words, k_scales, vT, vs, offs):
    idx = unstriped(offs)
    k = unpack_weight(k_words.reshape(D // 1024, 128, T, 2, 2).transpose(0, 3, 1, 2, 4).reshape(D // 512, 128, 2 * T), k_scales, "e2m1")
    v = f64(vT)
    pick = lambda x: x[:, idx].reshape(x.shape[0], B, N).transpose(1, 0, 2)
    q = f64(qT)
    score = mxq(q, 1, "e4m3").transpose(0, 2, 1) @ pick(k)
    m = score.max(-1, keepdims=True)
    p = np.exp(score - m)
    total = p.sum(-1, keepdims=True)
    w = p * pick(f64(vs))[:, :1, :]
    y = mxq(w, 2, "e4m3") @ mxq(pick(v).transpose(0, 2, 1), 1, "e4m3")
    y = y / total
    return y

@@ -1,0 +1,229 @@
+from contextlib import ExitStack
+
+import concourse.mybir as mybir
+from concourse.masks import make_identity
+
+B, N, T, D, DV, NQ = 2, 512, 2048, 1024, 256, 128
+FLOPS = 2 * B * NQ * N * (D + DV)
+
+F32 = mybir.dt.float32
+BF16 = mybir.dt.bfloat16
+I32 = mybir.dt.int32
+U32 = mybir.dt.uint32
+U16 = mybir.dt.uint16
+U8 = mybir.dt.uint8
+FP8X4 = mybir.dt.float8_e4m3fn_x4
+FP4X4 = mybir.dt.float4_e2m1fn_x4
+ACT = mybir.ActivationFunctionType
+ALU = mybir.AluOpType
+AX = mybir.AxisListType
+
+P = 128
+PACK = 4
+PASSES = D // (P * PACK)
+QUADS = 4
+LIST_COLS = N // 16
+FREE_ROWS = 32 - 4 * PASSES
+PLANE_ROWS = 32 * (QUADS - 1) + 4
+V_CHUNKS = 4
+V_CHUNK = T // V_CHUNKS
+
+
+def tile_attend_soft_kernel(tc, qT, k_words, k_scales, vT, vs, offs, out):
+    nc = tc.nc
+    with ExitStack() as ctx:
+        keep = ctx.enter_context(tc.tile_pool(name="keep", bufs=1))
+        psum = ctx.enter_context(tc.psum_pool(name="psum", bufs=1))
+
+        def sb(name, shape, dtype):
+            return keep.tile(shape, dtype, name=name, align_bytes=64)
+
+        offsets = keep.tile([P, B * LIST_COLS], U16, name="offsets")
+        nc.sync.dma_start(offsets[:], offs)
+
+        def slots(b):
+            return offsets[:, b * LIST_COLS : (b + 1) * LIST_COLS]
+
+        ks_pool = sb("ks_pool", [P, T], U8)
+        for quad in range(QUADS):
+            queue = nc.sync if quad < QUADS // 2 else nc.scalar
+            queue.dma_start(
+                ks_pool[32 * quad + FREE_ROWS : 32 * (quad + 1), :].bitcast(I32),
+                k_scales[:, 4 * quad : 4 * quad + 4, :].bitcast(I32),
+            )
+        for quad in range(QUADS):
+            nc.vector.memset(ks_pool[32 * quad : 32 * quad + FREE_ROWS, :].bitcast(I32), 0)
+
+        vs_pool = sb("vs_pool", [P, T], F32)
+        nc.scalar.dma_start(vs_pool[P - 1 : P, :], vs[0:1, :])
+        nc.vector.memset(vs_pool[0 : P - 1, :], 0.0)
+
+        zero = sb("zero", [P, 1], F32)
+        warm = sb("warm", [P, 1], F32)
+        nc.gpsimd.memset(zero[:], 0.0)
+        nc.scalar.activation(warm[:], zero[:], ACT.Exp)
+
+        kw_pool = sb("kw_pool", [P, T], I32)
+        nc.sync.dma_start(kw_pool[:], k_words[0].rearrange("p t c -> p (t c)").bitcast(I32))
+
+        q_raw = [sb("q_raw%d" % b, [P, PASSES, PACK, NQ], F32) for b in range(B)]
+        v_raw = [sb("v_raw%d" % c, [P, 2, V_CHUNK], F32) for c in range(V_CHUNKS)]
+        v_rows = vT.rearrange("(p h) t -> p h t", h=2)
+
+        def load_q(b):
+            nc.sync.dma_start(q_raw[b][:], qT[b].rearrange("(g p j) q -> p g j q", g=PASSES, j=PACK))
+
+        load_q(0)
+        for c in range(V_CHUNKS):
+            nc.sync.dma_start(v_raw[c][:], v_rows[:, :, c * V_CHUNK : (c + 1) * V_CHUNK])
+        load_q(1)
+
+        ident = sb("ident", [P, P], F32)
+        make_identity(nc, ident[:])
+
+
+        ks_got = sb("ks_got", [P, B * N], U8)
+        k_plane = [sb("k_plane%d" % g, [P, B * N], U8) for g in range(PASSES)]
+
+        def key_scales():
+            nc.vector.tensor_copy(ks_got[:], ks_pool[:].indirect(offsets[:]))
+            for g in range(PASSES):
+                nc.gpsimd.memset(k_plane[g][:].bitcast(I32), 0)
+                first = FREE_ROWS + 4 * g
+                nc.scalar.dma_start(
+                    k_plane[g][0:PLANE_ROWS, :].bitcast(I32), ks_got[first : first + PLANE_ROWS, :].bitcast(I32)
+                )
+
+        kw_got = [sb("kw_got%d" % b, [P, N], U32) for b in range(B)]
+        k_codes = [sb("k_codes%d" % b, [P, PASSES, N], U16) for b in range(B)]
+
+        def gather_keys(b):
+            nc.vector.tensor_copy(kw_got[b][:], kw_pool[:].bitcast(U32).indirect(slots(b)))
+            nc.vector.tensor_copy(k_codes[b][:], kw_got[b][:].bitcast(U16).rearrange("p (i o) -> p o i", o=PASSES))
+
+        q_bf = [sb("q_bf%d" % b, [P, PASSES, NQ, PACK], BF16) for b in range(B)]
+        q_codes = [sb("q_codes%d" % b, [P, PASSES * NQ], U32) for b in range(B)]
+        q_scale = [sb("q_scale%d" % b, [P, PASSES * NQ], U8) for b in range(B)]
+
+        def quantise_q(b):
+            for g in range(PASSES):
+                nc.scalar.copy(
+                    q_bf[b][:, g].rearrange("p (c i) j -> p c j i", i=4),
+                    q_raw[b][:, g].rearrange("p j (c i) -> p c j i", i=4),
+                )
+            nc.vector.quantize_mx(
+                out=q_codes[b][:].bitcast(FP8X4),
+                scales=q_scale[b][:],
+                in_=q_bf[b][:].rearrange("p g q j -> p (g q j)"),
+            )
+
+        score = [psum.tile([P, N], F32, name="score%d" % b) for b in range(B)]
+
+        def scores(b):
+            for g in range(PASSES):
+                nc.tensor.matmul_mx(
+                    out=score[b][:],
+                    lhsT=q_codes[b][:, g * NQ : (g + 1) * NQ].bitcast(FP8X4),
+                    lhsT_scale=q_scale[b][:, g * NQ : (g + 1) * NQ],
+                    rhs=k_codes[b][:, g, :].bitcast(FP4X4),
+                    rhs_scale=k_plane[g][:, b * N : (b + 1) * N],
+                    start=(g == 0),
+                    stop=(g == PASSES - 1),
+                )
+
+        vs_got = [sb("vs_got%d" % b, [P, N], F32) for b in range(B)]
+        vs_col = [sb("vs_col%d" % b, [P, PACK], F32) for b in range(B)]
+
+        def token_scales(b):
+            nc.vector.tensor_copy(vs_got[b][:], vs_pool[:].indirect(slots(b)))
+            turned = psum.tile([P, PACK, P], F32, name="turn%d" % b)
+            for j in range(PACK):
+                nc.tensor.transpose(turned[:, j, :], vs_got[b][:, j::PACK], ident[:])
+            nc.scalar.copy(vs_col[b][:], turned[:, :, P - 1])
+
+        v_pool = sb("v_pool", [P, T, 2], BF16)
+
+        def cast_values(c):
+            nc.scalar.activation(
+                v_pool[:, c * V_CHUNK : (c + 1) * V_CHUNK, :], v_raw[c][:].rearrange("p h t -> p t h"), ACT.Copy
+            )
+
+        v_got = [sb("v_got%d" % b, [P, N], U32) for b in range(B)]
+        v_bf = [sb("v_bf%d" % b, [P, DV, PACK], BF16) for b in range(B)]
+        v_codes = [sb("v_codes%d" % b, [P, DV], U32) for b in range(B)]
+        v_scale = [sb("v_scale%d" % b, [P, DV], U8) for b in range(B)]
+
+        def values(b):
+            window = v_pool[:].rearrange("p t h -> p (t h)").bitcast(U32)
+            nc.vector.tensor_copy(v_got[b][:], window.indirect(slots(b)))
+            turned = psum.tile([P, PACK, P], F32, name="v_turn%d" % b)
+            for j in range(PACK):
+                nc.tensor.transpose(turned[:, j, :], v_got[b][:].bitcast(F32)[:, j::PACK], ident[:])
+            nc.scalar.copy(v_bf[b][:], turned[:].bitcast(BF16).rearrange("s j e -> s e j"))
+            nc.vector.quantize_mx(
+                out=v_codes[b][:].bitcast(FP8X4), scales=v_scale[b][:], in_=v_bf[b][:].rearrange("s e j -> s (e j)")
+            )
+
+        neg_max = [sb("neg_max%d" % b, [P, 1], F32) for b in range(B)]
+        total = [sb("total%d" % b, [P, 1], F32) for b in range(B)]
+        inv_total = [sb("inv_total%d" % b, [P, 1], F32) for b in range(B)]
+        prob = [sb("prob%d" % b, [P, PACK, P], F32) for b in range(B)]
+        w_bf = [sb("w_bf%d" % b, [P, NQ, PACK], BF16) for b in range(B)]
+        w_codes = [sb("w_codes%d" % b, [P, NQ], U32) for b in range(B)]
+        w_scale = [sb("w_scale%d" % b, [P, NQ], U8) for b in range(B)]
+
+        def weights(b):
+            nc.vector.tensor_reduce(neg_max[b][:], score[b][:], AX.X, ALU.max, negate=True)
+            nc.scalar.activation(
+                prob[b][:],
+                score[b][:].rearrange("q (s j) -> q j s", j=PACK),
+                ACT.Exp,
+                bias=neg_max[b][:],
+                accum_out=total[b][:],
+            )
+            turned = psum.tile([P, PACK, P], F32, name="turn%d" % b)
+            for j in range(PACK):
+                nc.tensor.transpose(turned[:, j, :], prob[b][:, j, :], ident[:])
+            nc.vector.tensor_tensor(
+                w_bf[b][:],
+                turned[:].rearrange("s j q -> s q j"),
+                vs_col[b][:].unsqueeze(1).to_broadcast([P, NQ, PACK]),
+                ALU.mult,
+            )
+            nc.vector.quantize_mx(
+                out=w_codes[b][:].bitcast(FP8X4), scales=w_scale[b][:], in_=w_bf[b][:].rearrange("s q j -> s (q j)")
+            )
+            nc.vector.reciprocal(inv_total[b][:], total[b][:])
+
+        def finish(b):
+            acc = psum.tile([P, DV], F32, name="acc%d" % b)
+            nc.tensor.matmul_mx(
+                out=acc[:],
+                lhsT=w_codes[b][:].bitcast(FP8X4),
+                lhsT_scale=w_scale[b][:],
+                rhs=v_codes[b][:].bitcast(FP8X4),
+                rhs_scale=v_scale[b][:],
+                start=True,
+                stop=True,
+            )
+            result = sb("result%d" % b, [P, DV], F32)
+            nc.scalar.activation(result[:], acc[:], ACT.Copy, scale=inv_total[b][:])
+            nc.sync.dma_start(out[b], result[:])
+
+        key_scales()
+        token_scales(0)
+        token_scales(1)
+        gather_keys(0)
+        quantise_q(0)
+        scores(0)
+        gather_keys(1)
+        for c in range(V_CHUNKS):
+            cast_values(c)
+        weights(0)
+        values(0)
+        quantise_q(1)
+        scores(1)
+        values(1)
+        finish(0)
+        weights(1)
+        finish(1)

@@ -35,8 +35,8 @@ def tile_attend_soft_kernel(tc, qT, k_words, k_scales, vT, vs, offs, out):
         keep = ctx.enter_context(tc.tile_pool(name="keep", bufs=1))
         psum = ctx.enter_context(tc.psum_pool(name="psum", bufs=1))
 
-        def sb(name, shape, dtype):
-            return keep.tile(shape, dtype, name=name, align_bytes=64)
+        def sb(name, shape, dtype, tag=None):
+            return keep.tile(shape, dtype, name=name, tag=tag or name, align_bytes=64)
 
         offsets = keep.tile([P, B * LIST_COLS], U16, name="offsets")
         nc.sync.dma_start(offsets[:], offs)
@@ -56,7 +56,7 @@ def tile_attend_soft_kernel(tc, qT, k_words, k_scales, vT, vs, offs, out):
 
         vs_pool = sb("vs_pool", [P, T], F32)
         nc.scalar.dma_start(vs_pool[P - 1 : P, :], vs[0:1, :])
-        nc.vector.memset(vs_pool[0 : P - 1, :], 0.0)
+
 
         zero = sb("zero", [P, 1], F32)
         warm = sb("warm", [P, 1], F32)
@@ -64,7 +64,6 @@ def tile_attend_soft_kernel(tc, qT, k_words, k_scales, vT, vs, offs, out):
         nc.scalar.activation(warm[:], zero[:], ACT.Exp)
 
         kw_pool = sb("kw_pool", [P, T], I32)
-        nc.sync.dma_start(kw_pool[:], k_words[0].rearrange("p t c -> p (t c)").bitcast(I32))
 
         q_raw = [sb("q_raw%d" % b, [P, PASSES, PACK, NQ], F32) for b in range(B)]
         v_raw = [sb("v_raw%d" % c, [P, 2, V_CHUNK], F32) for c in range(V_CHUNKS)]
@@ -73,24 +72,28 @@ def tile_attend_soft_kernel(tc, qT, k_words, k_scales, vT, vs, offs, out):
         def load_q(b):
             nc.sync.dma_start(q_raw[b][:], qT[b].rearrange("(g p j) q -> p g j q", g=PASSES, j=PACK))
 
-        load_q(0)
-        for c in range(V_CHUNKS):
+        def load_v(c):
             nc.sync.dma_start(v_raw[c][:], v_rows[:, :, c * V_CHUNK : (c + 1) * V_CHUNK])
+
+        load_q(0)
         load_q(1)
+        nc.sync.dma_start(kw_pool[:], k_words[0].rearrange("p t c -> p (t c)").bitcast(I32))
+        load_v(0)
 
         ident = sb("ident", [P, P], F32)
         make_identity(nc, ident[:])
-
+        k_plane = [sb("k_plane%d" % g, [P, B * N], U8) for g in range(PASSES)]
+        for g in range(PASSES):
+            nc.gpsimd.memset(k_plane[g][:].bitcast(I32), 0)
+        nc.gpsimd.memset(vs_pool[0 : P - 1, :], 0.0)
 
         ks_got = sb("ks_got", [P, B * N], U8)
-        k_plane = [sb("k_plane%d" % g, [P, B * N], U8) for g in range(PASSES)]
 
         def key_scales():
             nc.vector.tensor_copy(ks_got[:], ks_pool[:].indirect(offsets[:]))
             for g in range(PASSES):
-                nc.gpsimd.memset(k_plane[g][:].bitcast(I32), 0)
                 first = FREE_ROWS + 4 * g
-                nc.scalar.dma_start(
+                nc.sync.dma_start(
                     k_plane[g][0:PLANE_ROWS, :].bitcast(I32), ks_got[first : first + PLANE_ROWS, :].bitcast(I32)
                 )
 
@@ -105,12 +108,14 @@ def tile_attend_soft_kernel(tc, qT, k_words, k_scales, vT, vs, offs, out):
         q_codes = [sb("q_codes%d" % b, [P, PASSES * NQ], U32) for b in range(B)]
         q_scale = [sb("q_scale%d" % b, [P, PASSES * NQ], U8) for b in range(B)]
 
-        def quantise_q(b):
+        def interleave_q(b):
             for g in range(PASSES):
                 nc.scalar.copy(
                     q_bf[b][:, g].rearrange("p (c i) j -> p c j i", i=4),
                     q_raw[b][:, g].rearrange("p j (c i) -> p c j i", i=4),
                 )
+
+        def quantise_q(b):
             nc.vector.quantize_mx(
                 out=q_codes[b][:].bitcast(FP8X4),
                 scales=q_scale[b][:],
@@ -131,15 +136,12 @@ def tile_attend_soft_kernel(tc, qT, k_words, k_scales, vT, vs, offs, out):
                     stop=(g == PASSES - 1),
                 )
 
-        vs_got = [sb("vs_got%d" % b, [P, N], F32) for b in range(B)]
         vs_col = [sb("vs_col%d" % b, [P, PACK], F32) for b in range(B)]
 
-        def token_scales(b):
-            nc.vector.tensor_copy(vs_got[b][:], vs_pool[:].indirect(slots(b)))
-            turned = psum.tile([P, PACK, P], F32, name="turn%d" % b)
-            for j in range(PACK):
-                nc.tensor.transpose(turned[:, j, :], vs_got[b][:, j::PACK], ident[:])
-            nc.scalar.copy(vs_col[b][:], turned[:, :, P - 1])
+        def token_scales(b, tag):
+            vs_got = sb("vs_got%d" % b, [P, N], F32, tag=tag)
+            nc.vector.tensor_copy(vs_got[:], vs_pool[:].indirect(slots(b)))
+            nc.sync.dma_start(vs_col[b][:], vs_got[P - 1 : P, :])
 
         v_pool = sb("v_pool", [P, T, 2], BF16)
 
@@ -153,9 +155,11 @@ def tile_attend_soft_kernel(tc, qT, k_words, k_scales, vT, vs, offs, out):
         v_codes = [sb("v_codes%d" % b, [P, DV], U32) for b in range(B)]
         v_scale = [sb("v_scale%d" % b, [P, DV], U8) for b in range(B)]
 
-        def values(b):
+        def gather_values(b):
             window = v_pool[:].rearrange("p t h -> p (t h)").bitcast(U32)
             nc.vector.tensor_copy(v_got[b][:], window.indirect(slots(b)))
+
+        def quantise_values(b):
             turned = psum.tile([P, PACK, P], F32, name="v_turn%d" % b)
             for j in range(PACK):
                 nc.tensor.transpose(turned[:, j, :], v_got[b][:].bitcast(F32)[:, j::PACK], ident[:])
@@ -167,23 +171,24 @@ def tile_attend_soft_kernel(tc, qT, k_words, k_scales, vT, vs, offs, out):
         neg_max = [sb("neg_max%d" % b, [P, 1], F32) for b in range(B)]
         total = [sb("total%d" % b, [P, 1], F32) for b in range(B)]
         inv_total = [sb("inv_total%d" % b, [P, 1], F32) for b in range(B)]
-        prob = [sb("prob%d" % b, [P, PACK, P], F32) for b in range(B)]
         w_bf = [sb("w_bf%d" % b, [P, NQ, PACK], BF16) for b in range(B)]
         w_codes = [sb("w_codes%d" % b, [P, NQ], U32) for b in range(B)]
         w_scale = [sb("w_scale%d" % b, [P, NQ], U8) for b in range(B)]
 
-        def weights(b):
+        def softmax(b, prob):
             nc.vector.tensor_reduce(neg_max[b][:], score[b][:], AX.X, ALU.max, negate=True)
             nc.scalar.activation(
-                prob[b][:],
+                prob[:, b],
                 score[b][:].rearrange("q (s j) -> q j s", j=PACK),
                 ACT.Exp,
                 bias=neg_max[b][:],
                 accum_out=total[b][:],
             )
+
+        def weights(b, prob):
             turned = psum.tile([P, PACK, P], F32, name="turn%d" % b)
             for j in range(PACK):
-                nc.tensor.transpose(turned[:, j, :], prob[b][:, j, :], ident[:])
+                nc.tensor.transpose(turned[:, j, :], prob[:, b, j, :], ident[:])
             nc.vector.tensor_tensor(
                 w_bf[b][:],
                 turned[:].rearrange("s j q -> s q j"),
@@ -210,20 +215,27 @@ def tile_attend_soft_kernel(tc, qT, k_words, k_scales, vT, vs, offs, out):
             nc.scalar.activation(result[:], acc[:], ACT.Copy, scale=inv_total[b][:])
             nc.sync.dma_start(out[b], result[:])
 
+        interleave_q(0)
+        interleave_q(1)
         key_scales()
-        token_scales(0)
-        token_scales(1)
-        gather_keys(0)
+        for c in range(1, V_CHUNKS):
+            load_v(c)
+        token_scales(0, "vs_got0")
         quantise_q(0)
-        scores(0)
-        gather_keys(1)
+        quantise_q(1)
+        for b in range(B):
+            gather_keys(b)
+            scores(b)
+        token_scales(1, "kw_got1")
         for c in range(V_CHUNKS):
             cast_values(c)
-        weights(0)
-        values(0)
-        quantise_q(1)
-        scores(1)
-        values(1)
-        finish(0)
-        weights(1)
-        finish(1)
+        prob = sb("prob", [P, B, PACK, P], F32, tag="v_raw%d" % (V_CHUNKS - 1))
+        for b in range(B):
+            softmax(b, prob)
+        for b in range(B):
+            gather_values(b)
+        for b in range(B):
+            weights(b, prob)
+        for b in range(B):
+            quantise_values(b)
+            finish(b)

@@ -23,10 +23,10 @@ PACK = 4
 PASSES = D // (P * PACK)
 QUADS = 4
 LIST_COLS = N // 16
-FREE_ROWS = 32 - 4 * PASSES
-PLANE_ROWS = 32 * (QUADS - 1) + 4
-V_CHUNKS = 4
-V_CHUNK = T // V_CHUNKS
+KS_FIRST = P - 16 * PASSES
+V_EDGES = (0, 640, 1280, 1728, T)
+V_CHUNKS = len(V_EDGES) - 1
+V_EARLY = 2
 
 
 def tile_attend_soft_kernel(tc, qT, k_words, k_scales, vT, vs, offs, out):
@@ -45,64 +45,55 @@ def tile_attend_soft_kernel(tc, qT, k_words, k_scales, vT, vs, offs, out):
             return offsets[:, b * LIST_COLS : (b + 1) * LIST_COLS]
 
         ks_pool = sb("ks_pool", [P, T], U8)
-        for quad in range(QUADS):
-            queue = nc.sync if quad < QUADS // 2 else nc.scalar
-            queue.dma_start(
-                ks_pool[32 * quad + FREE_ROWS : 32 * (quad + 1), :].bitcast(I32),
-                k_scales[:, 4 * quad : 4 * quad + 4, :].bitcast(I32),
-            )
-        for quad in range(QUADS):
-            nc.vector.memset(ks_pool[32 * quad : 32 * quad + FREE_ROWS, :].bitcast(I32), 0)
+        nc.sync.dma_start(ks_pool[KS_FIRST:P, :].bitcast(I32), k_scales.rearrange("g f t -> f g t").bitcast(I32))
+        nc.vector.memset(ks_pool[0:KS_FIRST, :].bitcast(I32), 0)
 
         vs_pool = sb("vs_pool", [P, T], F32)
         nc.scalar.dma_start(vs_pool[P - 1 : P, :], vs[0:1, :])
-
-
-        zero = sb("zero", [P, 1], F32)
-        warm = sb("warm", [P, 1], F32)
-        nc.gpsimd.memset(zero[:], 0.0)
-        nc.scalar.activation(warm[:], zero[:], ACT.Exp)
+        nc.vector.memset(vs_pool[0 : P - 1, :], 0.0)
 
         kw_pool = sb("kw_pool", [P, T], I32)
 
         q_raw = [sb("q_raw%d" % b, [P, PASSES, PACK, NQ], F32) for b in range(B)]
-        v_raw = [sb("v_raw%d" % c, [P, 2, V_CHUNK], F32) for c in range(V_CHUNKS)]
+        v_raw = [sb("v_raw%d" % c, [P, 2, V_EDGES[c + 1] - V_EDGES[c]], F32) for c in range(V_CHUNKS)]
         v_rows = vT.rearrange("(p h) t -> p h t", h=2)
 
         def load_q(b):
             nc.sync.dma_start(q_raw[b][:], qT[b].rearrange("(g p j) q -> p g j q", g=PASSES, j=PACK))
 
         def load_v(c):
-            nc.sync.dma_start(v_raw[c][:], v_rows[:, :, c * V_CHUNK : (c + 1) * V_CHUNK])
+            nc.sync.dma_start(v_raw[c][:], v_rows[:, :, V_EDGES[c] : V_EDGES[c + 1]])
 
         load_q(0)
         load_q(1)
         nc.sync.dma_start(kw_pool[:], k_words[0].rearrange("p t c -> p (t c)").bitcast(I32))
-        load_v(0)
+        for c in range(V_EARLY):
+            load_v(c)
 
         ident = sb("ident", [P, P], F32)
         make_identity(nc, ident[:])
-        k_plane = [sb("k_plane%d" % g, [P, B * N], U8) for g in range(PASSES)]
-        for g in range(PASSES):
-            nc.gpsimd.memset(k_plane[g][:].bitcast(I32), 0)
-        nc.gpsimd.memset(vs_pool[0 : P - 1, :], 0.0)
+        k_plane = sb("k_plane", [P, PASSES, B * N], U8)
 
         ks_got = sb("ks_got", [P, B * N], U8)
 
         def key_scales():
             nc.vector.tensor_copy(ks_got[:], ks_pool[:].indirect(offsets[:]))
-            for g in range(PASSES):
-                first = FREE_ROWS + 4 * g
+            for quad in range(QUADS):
+                first = KS_FIRST + 4 * PASSES * quad
                 nc.sync.dma_start(
-                    k_plane[g][0:PLANE_ROWS, :].bitcast(I32), ks_got[first : first + PLANE_ROWS, :].bitcast(I32)
+                    k_plane[32 * quad : 32 * quad + 4].bitcast(I32),
+                    ks_got[first : first + 4 * PASSES, :].bitcast(I32),
                 )
 
-        kw_got = [sb("kw_got%d" % b, [P, N], U32) for b in range(B)]
+        kw_got = sb("kw_got", [P, B * N], U32)
         k_codes = [sb("k_codes%d" % b, [P, PASSES, N], U16) for b in range(B)]
 
-        def gather_keys(b):
-            nc.vector.tensor_copy(kw_got[b][:], kw_pool[:].bitcast(U32).indirect(slots(b)))
-            nc.vector.tensor_copy(k_codes[b][:], kw_got[b][:].bitcast(U16).rearrange("p (i o) -> p o i", o=PASSES))
+        def gather_keys():
+            nc.vector.tensor_copy(kw_got[:], kw_pool[:].bitcast(U32).indirect(offsets[:]))
+
+        def part_keys(b):
+            pairs = kw_got[:, b * N : (b + 1) * N].bitcast(U16)
+            nc.vector.tensor_copy(k_codes[b][:], pairs.rearrange("p (i o) -> p o i", o=PASSES))
 
         q_bf = [sb("q_bf%d" % b, [P, PASSES, NQ, PACK], BF16) for b in range(B)]
         q_codes = [sb("q_codes%d" % b, [P, PASSES * NQ], U32) for b in range(B)]
@@ -122,7 +113,7 @@ def tile_attend_soft_kernel(tc, qT, k_words, k_scales, vT, vs, offs, out):
                 in_=q_bf[b][:].rearrange("p g q j -> p (g q j)"),
             )
 
-        score = [psum.tile([P, N], F32, name="score%d" % b) for b in range(B)]
+        score = [psum.tile([P, N], F32, name="score%d" % b, tag="score%d" % b) for b in range(B)]
 
         def scores(b):
             for g in range(PASSES):
@@ -131,7 +122,7 @@ def tile_attend_soft_kernel(tc, qT, k_words, k_scales, vT, vs, offs, out):
                     lhsT=q_codes[b][:, g * NQ : (g + 1) * NQ].bitcast(FP8X4),
                     lhsT_scale=q_scale[b][:, g * NQ : (g + 1) * NQ],
                     rhs=k_codes[b][:, g, :].bitcast(FP4X4),
-                    rhs_scale=k_plane[g][:, b * N : (b + 1) * N],
+                    rhs_scale=k_plane[:, g, b * N : (b + 1) * N],
                     start=(g == 0),
                     stop=(g == PASSES - 1),
                 )
@@ -147,7 +138,7 @@ def tile_attend_soft_kernel(tc, qT, k_words, k_scales, vT, vs, offs, out):
 
         def cast_values(c):
             nc.scalar.activation(
-                v_pool[:, c * V_CHUNK : (c + 1) * V_CHUNK, :], v_raw[c][:].rearrange("p h t -> p t h"), ACT.Copy
+                v_pool[:, V_EDGES[c] : V_EDGES[c + 1], :], v_raw[c][:].rearrange("p h t -> p t h"), ACT.Copy
             )
 
         v_got = [sb("v_got%d" % b, [P, N], U32) for b in range(B)]
@@ -160,7 +151,7 @@ def tile_attend_soft_kernel(tc, qT, k_words, k_scales, vT, vs, offs, out):
             nc.vector.tensor_copy(v_got[b][:], window.indirect(slots(b)))
 
         def quantise_values(b):
-            turned = psum.tile([P, PACK, P], F32, name="v_turn%d" % b)
+            turned = psum.tile([P, PACK, P], F32, name="v_turn%d" % b, tag="score%d" % b)
             for j in range(PACK):
                 nc.tensor.transpose(turned[:, j, :], v_got[b][:].bitcast(F32)[:, j::PACK], ident[:])
             nc.scalar.copy(v_bf[b][:], turned[:].bitcast(BF16).rearrange("s j e -> s e j"))
@@ -169,8 +160,8 @@ def tile_attend_soft_kernel(tc, qT, k_words, k_scales, vT, vs, offs, out):
             )
 
         neg_max = [sb("neg_max%d" % b, [P, 1], F32) for b in range(B)]
-        total = [sb("total%d" % b, [P, 1], F32) for b in range(B)]
-        inv_total = [sb("inv_total%d" % b, [P, 1], F32) for b in range(B)]
+        total = sb("total", [P, B], F32)
+        inv_total = sb("inv_total", [P, B], F32)
         w_bf = [sb("w_bf%d" % b, [P, NQ, PACK], BF16) for b in range(B)]
         w_codes = [sb("w_codes%d" % b, [P, NQ], U32) for b in range(B)]
         w_scale = [sb("w_scale%d" % b, [P, NQ], U8) for b in range(B)]
@@ -182,7 +173,7 @@ def tile_attend_soft_kernel(tc, qT, k_words, k_scales, vT, vs, offs, out):
                 score[b][:].rearrange("q (s j) -> q j s", j=PACK),
                 ACT.Exp,
                 bias=neg_max[b][:],
-                accum_out=total[b][:],
+                accum_out=total[:, b : b + 1],
             )
 
         def weights(b, prob):
@@ -198,7 +189,6 @@ def tile_attend_soft_kernel(tc, qT, k_words, k_scales, vT, vs, offs, out):
             nc.vector.quantize_mx(
                 out=w_codes[b][:].bitcast(FP8X4), scales=w_scale[b][:], in_=w_bf[b][:].rearrange("s q j -> s (q j)")
             )
-            nc.vector.reciprocal(inv_total[b][:], total[b][:])
 
         def finish(b):
             acc = psum.tile([P, DV], F32, name="acc%d" % b)
@@ -212,21 +202,22 @@ def tile_attend_soft_kernel(tc, qT, k_words, k_scales, vT, vs, offs, out):
                 stop=True,
             )
             result = sb("result%d" % b, [P, DV], F32)
-            nc.scalar.activation(result[:], acc[:], ACT.Copy, scale=inv_total[b][:])
+            nc.scalar.activation(result[:], acc[:], ACT.Copy, scale=inv_total[:, b : b + 1])
             nc.sync.dma_start(out[b], result[:])
 
         interleave_q(0)
         interleave_q(1)
         key_scales()
-        for c in range(1, V_CHUNKS):
+        for c in range(V_EARLY, V_CHUNKS):
             load_v(c)
         token_scales(0, "vs_got0")
         quantise_q(0)
         quantise_q(1)
+        gather_keys()
         for b in range(B):
-            gather_keys(b)
+            part_keys(b)
             scores(b)
-        token_scales(1, "kw_got1")
+        token_scales(1, "ks_got")
         for c in range(V_CHUNKS):
             cast_values(c)
         prob = sb("prob", [P, B, PACK, P], F32, tag="v_raw%d" % (V_CHUNKS - 1))
@@ -234,8 +225,9 @@ def tile_attend_soft_kernel(tc, qT, k_words, k_scales, vT, vs, offs, out):
             softmax(b, prob)
         for b in range(B):
             gather_values(b)
+        nc.vector.reciprocal(inv_total[:], total[:])
         for b in range(B):
             weights(b, prob)
-        for b in range(B):
             quantise_values(b)
+        for b in range(B):
             finish(b)

@@ -27,6 +27,8 @@ KS_FIRST = P - 16 * PASSES
 V_EDGES = (0, 640, 1280, 1728, T)
 V_CHUNKS = len(V_EDGES) - 1
 V_EARLY = 2
+HALVES = 2
+HALF = DV // HALVES
 
 
 def tile_attend_soft_kernel(tc, qT, k_words, k_scales, vT, vs, offs, out):
@@ -65,8 +67,8 @@ def tile_attend_soft_kernel(tc, qT, k_words, k_scales, vT, vs, offs, out):
             nc.sync.dma_start(v_raw[c][:], v_rows[:, :, V_EDGES[c] : V_EDGES[c + 1]])
 
         load_q(0)
-        load_q(1)
         nc.sync.dma_start(kw_pool[:], k_words[0].rearrange("p t c -> p (t c)").bitcast(I32))
+        load_q(1)
         for c in range(V_EARLY):
             load_v(c)
 
@@ -154,10 +156,15 @@ def tile_attend_soft_kernel(tc, qT, k_words, k_scales, vT, vs, offs, out):
             turned = psum.tile([P, PACK, P], F32, name="v_turn%d" % b, tag="score%d" % b)
             for j in range(PACK):
                 nc.tensor.transpose(turned[:, j, :], v_got[b][:].bitcast(F32)[:, j::PACK], ident[:])
-            nc.scalar.copy(v_bf[b][:], turned[:].bitcast(BF16).rearrange("s j e -> s e j"))
-            nc.vector.quantize_mx(
-                out=v_codes[b][:].bitcast(FP8X4), scales=v_scale[b][:], in_=v_bf[b][:].rearrange("s e j -> s (e j)")
-            )
+            by_feature = turned[:].bitcast(BF16).rearrange("s j e -> s e j")
+            for h in range(HALVES):
+                cols = slice(h * HALF, (h + 1) * HALF)
+                nc.scalar.copy(v_bf[b][:, cols, :], by_feature[:, cols, :])
+                nc.vector.quantize_mx(
+                    out=v_codes[b][:, cols].bitcast(FP8X4),
+                    scales=v_scale[b][:, cols],
+                    in_=v_bf[b][:, cols, :].rearrange("s e j -> s (e j)"),
+                )
 
         neg_max = [sb("neg_max%d" % b, [P, 1], F32) for b in range(B)]
         total = sb("total", [P, B], F32)
@@ -190,20 +197,21 @@ def tile_attend_soft_kernel(tc, qT, k_words, k_scales, vT, vs, offs, out):
                 out=w_codes[b][:].bitcast(FP8X4), scales=w_scale[b][:], in_=w_bf[b][:].rearrange("s q j -> s (q j)")
             )
 
-        def finish(b):
-            acc = psum.tile([P, DV], F32, name="acc%d" % b)
+        def finish(b, h):
+            cols = slice(h * HALF, (h + 1) * HALF)
+            acc = psum.tile([P, HALF], F32, name="acc%d_%d" % (b, h))
             nc.tensor.matmul_mx(
                 out=acc[:],
                 lhsT=w_codes[b][:].bitcast(FP8X4),
                 lhsT_scale=w_scale[b][:],
-                rhs=v_codes[b][:].bitcast(FP8X4),
-                rhs_scale=v_scale[b][:],
+                rhs=v_codes[b][:, cols].bitcast(FP8X4),
+                rhs_scale=v_scale[b][:, cols],
                 start=True,
                 stop=True,
             )
-            result = sb("result%d" % b, [P, DV], F32)
+            result = sb("result%d_%d" % (b, h), [P, HALF], F32)
             nc.scalar.activation(result[:], acc[:], ACT.Copy, scale=inv_total[:, b : b + 1])
-            nc.sync.dma_start(out[b], result[:])
+            nc.sync.dma_start(out[b, :, cols], result[:])
 
         interleave_q(0)
         interleave_q(1)
@@ -212,8 +220,8 @@ def tile_attend_soft_kernel(tc, qT, k_words, k_scales, vT, vs, offs, out):
             load_v(c)
         token_scales(0, "vs_got0")
         quantise_q(0)
-        quantise_q(1)
         gather_keys()
+        quantise_q(1)
         for b in range(B):
             part_keys(b)
             scores(b)
@@ -230,4 +238,5 @@ def tile_attend_soft_kernel(tc, qT, k_words, k_scales, vT, vs, offs, out):
             weights(b, prob)
             quantise_values(b)
         for b in range(B):
-            finish(b)
+            for h in range(HALVES):
+                finish(b, h)

from contextlib import ExitStack

import concourse.mybir as mybir
from concourse.masks import make_identity

B, N, T, D, DV, NQ = 2, 512, 2048, 1024, 256, 128
FLOPS = 2 * B * NQ * N * (D + DV)

F32 = mybir.dt.float32
BF16 = mybir.dt.bfloat16
I32 = mybir.dt.int32
U32 = mybir.dt.uint32
U16 = mybir.dt.uint16
U8 = mybir.dt.uint8
FP8X4 = mybir.dt.float8_e4m3fn_x4
FP4X4 = mybir.dt.float4_e2m1fn_x4
ACT = mybir.ActivationFunctionType
ALU = mybir.AluOpType
AX = mybir.AxisListType

P = 128
PACK = 4
PASSES = D // (P * PACK)
QUADS = 4
LIST_COLS = N // 16
KS_FIRST = P - 16 * PASSES
V_EDGES = (0, 640, 1280, 1728, T)
V_CHUNKS = len(V_EDGES) - 1
V_EARLY = 2
HALVES = 2
HALF = DV // HALVES


def tile_attend_soft_kernel(tc, qT, k_words, k_scales, vT, vs, offs, out):
    nc = tc.nc
    with ExitStack() as ctx:
        keep = ctx.enter_context(tc.tile_pool(name="keep", bufs=1))
        psum = ctx.enter_context(tc.psum_pool(name="psum", bufs=1))

        def sb(name, shape, dtype, tag=None):
            return keep.tile(shape, dtype, name=name, tag=tag or name, align_bytes=64)

        offsets = keep.tile([P, B * LIST_COLS], U16, name="offsets")
        nc.sync.dma_start(offsets[:], offs)

        def slots(b):
            return offsets[:, b * LIST_COLS : (b + 1) * LIST_COLS]

        ks_pool = sb("ks_pool", [P, T], U8)
        nc.sync.dma_start(ks_pool[KS_FIRST:P, :].bitcast(I32), k_scales.rearrange("g f t -> f g t").bitcast(I32))
        nc.vector.memset(ks_pool[0:KS_FIRST, :].bitcast(I32), 0)

        vs_pool = sb("vs_pool", [P, T], F32)
        nc.scalar.dma_start(vs_pool[P - 1 : P, :], vs[0:1, :])
        nc.vector.memset(vs_pool[0 : P - 1, :], 0.0)

        kw_pool = sb("kw_pool", [P, T], I32)

        q_raw = [sb("q_raw%d" % b, [P, PASSES, PACK, NQ], F32) for b in range(B)]
        v_raw = [sb("v_raw%d" % c, [P, 2, V_EDGES[c + 1] - V_EDGES[c]], F32) for c in range(V_CHUNKS)]
        v_rows = vT.rearrange("(p h) t -> p h t", h=2)

        def load_q(b):
            nc.sync.dma_start(q_raw[b][:], qT[b].rearrange("(g p j) q -> p g j q", g=PASSES, j=PACK))

        def load_v(c):
            nc.sync.dma_start(v_raw[c][:], v_rows[:, :, V_EDGES[c] : V_EDGES[c + 1]])

        load_q(0)
        nc.sync.dma_start(kw_pool[:], k_words[0].rearrange("p t c -> p (t c)").bitcast(I32))
        load_q(1)
        for c in range(V_EARLY):
            load_v(c)

        ident = sb("ident", [P, P], F32)
        make_identity(nc, ident[:])
        k_plane = sb("k_plane", [P, PASSES, B * N], U8)

        ks_got = sb("ks_got", [P, B * N], U8)

        def key_scales():
            nc.vector.tensor_copy(ks_got[:], ks_pool[:].indirect(offsets[:]))
            for quad in range(QUADS):
                first = KS_FIRST + 4 * PASSES * quad
                nc.sync.dma_start(
                    k_plane[32 * quad : 32 * quad + 4].bitcast(I32),
                    ks_got[first : first + 4 * PASSES, :].bitcast(I32),
                )

        kw_got = sb("kw_got", [P, B * N], U32)
        k_codes = [sb("k_codes%d" % b, [P, PASSES, N], U16) for b in range(B)]

        def gather_keys():
            nc.vector.tensor_copy(kw_got[:], kw_pool[:].bitcast(U32).indirect(offsets[:]))

        def part_keys(b):
            pairs = kw_got[:, b * N : (b + 1) * N].bitcast(U16)
            nc.vector.tensor_copy(k_codes[b][:], pairs.rearrange("p (i o) -> p o i", o=PASSES))

        q_bf = [sb("q_bf%d" % b, [P, PASSES, NQ, PACK], BF16) for b in range(B)]
        q_codes = [sb("q_codes%d" % b, [P, PASSES * NQ], U32) for b in range(B)]
        q_scale = [sb("q_scale%d" % b, [P, PASSES * NQ], U8) for b in range(B)]

        def interleave_q(b):
            for g in range(PASSES):
                nc.scalar.copy(
                    q_bf[b][:, g].rearrange("p (c i) j -> p c j i", i=4),
                    q_raw[b][:, g].rearrange("p j (c i) -> p c j i", i=4),
                )

        def quantise_q(b):
            nc.vector.quantize_mx(
                out=q_codes[b][:].bitcast(FP8X4),
                scales=q_scale[b][:],
                in_=q_bf[b][:].rearrange("p g q j -> p (g q j)"),
            )

        score = [psum.tile([P, N], F32, name="score%d" % b, tag="score%d" % b) for b in range(B)]

        def scores(b):
            for g in range(PASSES):
                nc.tensor.matmul_mx(
                    out=score[b][:],
                    lhsT=q_codes[b][:, g * NQ : (g + 1) * NQ].bitcast(FP8X4),
                    lhsT_scale=q_scale[b][:, g * NQ : (g + 1) * NQ],
                    rhs=k_codes[b][:, g, :].bitcast(FP4X4),
                    rhs_scale=k_plane[:, g, b * N : (b + 1) * N],
                    start=(g == 0),
                    stop=(g == PASSES - 1),
                )

        vs_col = [sb("vs_col%d" % b, [P, PACK], F32) for b in range(B)]

        def token_scales(b, tag):
            vs_got = sb("vs_got%d" % b, [P, N], F32, tag=tag)
            nc.vector.tensor_copy(vs_got[:], vs_pool[:].indirect(slots(b)))
            nc.sync.dma_start(vs_col[b][:], vs_got[P - 1 : P, :])

        v_pool = sb("v_pool", [P, T, 2], BF16)

        def cast_values(c):
            nc.scalar.activation(
                v_pool[:, V_EDGES[c] : V_EDGES[c + 1], :], v_raw[c][:].rearrange("p h t -> p t h"), ACT.Copy
            )

        v_got = [sb("v_got%d" % b, [P, N], U32) for b in range(B)]
        v_bf = [sb("v_bf%d" % b, [P, DV, PACK], BF16) for b in range(B)]
        v_codes = [sb("v_codes%d" % b, [P, DV], U32) for b in range(B)]
        v_scale = [sb("v_scale%d" % b, [P, DV], U8) for b in range(B)]

        def gather_values(b):
            window = v_pool[:].rearrange("p t h -> p (t h)").bitcast(U32)
            nc.vector.tensor_copy(v_got[b][:], window.indirect(slots(b)))

        def quantise_values(b):
            turned = psum.tile([P, PACK, P], F32, name="v_turn%d" % b, tag="score%d" % b)
            for j in range(PACK):
                nc.tensor.transpose(turned[:, j, :], v_got[b][:].bitcast(F32)[:, j::PACK], ident[:])
            by_feature = turned[:].bitcast(BF16).rearrange("s j e -> s e j")
            for h in range(HALVES):
                cols = slice(h * HALF, (h + 1) * HALF)
                nc.scalar.copy(v_bf[b][:, cols, :], by_feature[:, cols, :])
                nc.vector.quantize_mx(
                    out=v_codes[b][:, cols].bitcast(FP8X4),
                    scales=v_scale[b][:, cols],
                    in_=v_bf[b][:, cols, :].rearrange("s e j -> s (e j)"),
                )

        neg_max = [sb("neg_max%d" % b, [P, 1], F32) for b in range(B)]
        total = sb("total", [P, B], F32)
        inv_total = sb("inv_total", [P, B], F32)
        w_bf = [sb("w_bf%d" % b, [P, NQ, PACK], BF16) for b in range(B)]
        w_codes = [sb("w_codes%d" % b, [P, NQ], U32) for b in range(B)]
        w_scale = [sb("w_scale%d" % b, [P, NQ], U8) for b in range(B)]

        def softmax(b, prob):
            nc.vector.tensor_reduce(neg_max[b][:], score[b][:], AX.X, ALU.max, negate=True)
            nc.scalar.activation(
                prob[:, b],
                score[b][:].rearrange("q (s j) -> q j s", j=PACK),
                ACT.Exp,
                bias=neg_max[b][:],
                accum_out=total[:, b : b + 1],
            )

        def weights(b, prob):
            turned = psum.tile([P, PACK, P], F32, name="turn%d" % b)
            for j in range(PACK):
                nc.tensor.transpose(turned[:, j, :], prob[:, b, j, :], ident[:])
            nc.vector.tensor_tensor(
                w_bf[b][:],
                turned[:].rearrange("s j q -> s q j"),
                vs_col[b][:].unsqueeze(1).to_broadcast([P, NQ, PACK]),
                ALU.mult,
            )
            nc.vector.quantize_mx(
                out=w_codes[b][:].bitcast(FP8X4), scales=w_scale[b][:], in_=w_bf[b][:].rearrange("s q j -> s (q j)")
            )

        def finish(b, h):
            cols = slice(h * HALF, (h + 1) * HALF)
            acc = psum.tile([P, HALF], F32, name="acc%d_%d" % (b, h))
            nc.tensor.matmul_mx(
                out=acc[:],
                lhsT=w_codes[b][:].bitcast(FP8X4),
                lhsT_scale=w_scale[b][:],
                rhs=v_codes[b][:, cols].bitcast(FP8X4),
                rhs_scale=v_scale[b][:, cols],
                start=True,
                stop=True,
            )
            result = sb("result%d_%d" % (b, h), [P, HALF], F32)
            nc.scalar.activation(result[:], acc[:], ACT.Copy, scale=inv_total[:, b : b + 1])
            nc.sync.dma_start(out[b, :, cols], result[:])

        interleave_q(0)
        interleave_q(1)
        key_scales()
        for c in range(V_EARLY, V_CHUNKS):
            load_v(c)
        token_scales(0, "vs_got0")
        quantise_q(0)
        gather_keys()
        quantise_q(1)
        for b in range(B):
            part_keys(b)
            scores(b)
        token_scales(1, "ks_got")
        for c in range(V_CHUNKS):
            cast_values(c)
        prob = sb("prob", [P, B, PACK, P], F32, tag="v_raw%d" % (V_CHUNKS - 1))
        for b in range(B):
            softmax(b, prob)
        for b in range(B):
            gather_values(b)
        nc.vector.reciprocal(inv_total[:], total[:])
        for b in range(B):
            weights(b, prob)
            quantise_values(b)
        for b in range(B):
            for h in range(HALVES):
                finish(b, h)
